import numpy as np
import ml_dtypes


def mxq(x, axis, fmt="e4m3"):
    dtype, down = {"e4m3": (ml_dtypes.float8_e4m3fn, 7), "e5m2": (ml_dtypes.float8_e5m2, 14)}[fmt]
    v = np.moveaxis(np.asarray(x, np.float32).astype(ml_dtypes.bfloat16).astype(np.float64), axis, -1)
    blocks = v.reshape(v.shape[:-1] + (-1, 32))
    amax = np.abs(blocks).max(-1, keepdims=True)
    byte = np.maximum(np.where(amax > 0, np.frexp(amax)[1] - 1 + 127, 0) - down, 1)
    scale = np.exp2(byte - 127.0)
    codes = (blocks / scale).astype(np.float32).astype(dtype).astype(np.float64)
    return np.moveaxis((codes * scale).reshape(v.shape), -1, axis)


WIDE = False


def mx_kscale(k):
    if not WIDE:
        return np.ones(k)
    levels = np.array([10, -10, 5, -5, 0])
    if k % 512:
        return np.exp2(np.random.permutation(np.resize(levels, k // 32))).repeat(32)
    a = np.empty((k // 512, 16))
    for p in range(k // 512):
        a[p, :8] = np.random.permutation(np.resize(levels, 8))
        for g in range(8):
            far = levels[np.abs(levels - a[p, g]) >= 10]
            a[p, g + 8] = far[np.random.randint(len(far))]
    return np.exp2(a.ravel()).repeat(32)


def f64(x):
    return np.asarray(x).astype(np.float64)


def striped(idx):
    return np.tile(np.asarray(idx).reshape(-1, 16).T, (8, 1)).astype(np.uint16)


def unstriped(offs):
    return offs[:16].T.reshape(-1).astype(np.int64)


B, N, T, D, DV, NQ = 2, 512, 2048, 512, 512, 128
PAGE = 64


def setup_inputs():
    n = np.random.standard_normal
    pages = np.random.permutation(T // PAGE)[:B * N // PAGE]
    idx = (pages[:, None] * PAGE + np.arange(PAGE)[None, :]).reshape(-1)
    s = mx_kscale(D)[:, None]
    u = np.ones(T)
    u[idx] = mx_kscale(B * N)
    r = np.random.uniform(0.5, 2.0, T)
    raw = n((D, T)) / s / (u * r)
    return {
        "qT": (n((B, D, NQ)) * s * (1.00 / np.sqrt(D))).astype(np.float32),
        "cT": raw.astype(np.float32),
        "ts": np.tile(u * r, (128, 1)).astype(np.float32),
        "ch": np.tile(s[:, 0] * np.random.uniform(0.5, 2.0, D), (128, 1)).astype(np.float32),
        "offs": striped(idx),
    }


def reference(qT, cT, ts, ch, offs):
    idx = unstriped(offs)
    c = f64(cT)
    pick = lambda x: x[:, idx].reshape(x.shape[0], B, N).transpose(1, 0, 2)
    q = f64(qT)
    score = mxq(q, 1, "e4m3").transpose(0, 2, 1) @ mxq(pick(c), 1, "e4m3")
    score = score * pick(f64(ts))[:, :1, :]
    m = score.max(-1, keepdims=True)
    p = np.exp(score - m)
    total = p.sum(-1, keepdims=True)
    w = p * pick(f64(ts))[:, :1, :]
    y = mxq(w, 2, "e4m3") @ mxq(pick(c).transpose(0, 2, 1), 1, "e4m3")
    y = y / total
    y = y * f64(ch)[:1]
    return y

@@ -1,0 +1,246 @@
+from contextlib import ExitStack
+
+import concourse.mybir as mybir
+from concourse.masks import make_identity
+
+B, N, T, D, DV, NQ = 2, 512, 2048, 512, 512, 128
+P = 128
+PACK = 4
+FLOPS = 2 * B * NQ * N * (D + DV)
+
+F32 = mybir.dt.float32
+BF16 = mybir.dt.bfloat16
+U32 = mybir.dt.uint32
+U16 = mybir.dt.uint16
+U8 = mybir.dt.uint8
+FP8X4 = mybir.dt.float8_e4m3fn_x4
+ACT = mybir.ActivationFunctionType
+ALU = mybir.AluOpType
+
+CHUNKS = [(0, 0, 1024, 512), (0, 1024, 1024, 512), (1, 0, 1024, 512), (1, 1024, 512, 256), (1, 1536, 256, 128), (1, 1792, 256, 160)]
+
+
+def tile_attend_mla_kernel(tc, qT, cT, ts, ch, offs, out):
+    nc = tc.nc
+    with ExitStack() as ctx:
+        keep = ctx.enter_context(tc.tile_pool(name="keep", bufs=1))
+        stage = ctx.enter_context(tc.tile_pool(name="stage", bufs=2))
+        psum = ctx.enter_context(tc.psum_pool(name="psum", bufs=1))
+
+        offsets = keep.tile([P, B * N // 16], U16, name="offsets")
+        nc.sync.dma_start(offsets[:], offs)
+        pool_rows = cT.rearrange("(p t) n -> p t n", t=PACK)
+        raw = []
+        for i, (u, c0, w, wv) in enumerate(CHUNKS):
+            r = keep.tile([P, 2, w], F32, name=f"raw{i}")
+            nc.sync.dma_start(out=r[:], in_=pool_rows[:, 2 * u : 2 * u + 2, c0 : c0 + w])
+            raw.append(r)
+        q_raw = keep.tile([P, B, PACK, NQ], F32, name="q_raw")
+        nc.sync.dma_start(out=q_raw[:], in_=qT.rearrange("b (p t) q -> p b t q", t=PACK))
+        ts_sb = keep.tile([P, T], F32, name="ts_sb")
+        nc.sync.dma_start(out=ts_sb[:], in_=ts)
+        ch_sb = keep.tile([P, DV], F32, name="ch_sb")
+        nc.sync.dma_start(out=ch_sb[:], in_=ch)
+
+        ident_b = keep.tile([P, P], BF16, name="ident_b")
+        make_identity(nc, ident_b[:])
+        ident_f = keep.tile([P, P], F32, name="ident_f")
+        make_identity(nc, ident_f[:])
+        warm = keep.tile([P, 1], F32, name="warm")
+        nc.gpsimd.memset(warm[:], 0.0)
+        warm2 = keep.tile([P, 1], F32, name="warm2")
+        nc.scalar.activation(out=warm2[:], in_=warm[:], func=ACT.Exp)
+
+        words = [keep.tile([P, T, 2], BF16, name=f"words{u}") for u in range(2)]
+        keys = [keep.tile([P, N * PACK], BF16, name=f"keys{b}", align_bytes=64) for b in range(B)]
+        kq = [keep.tile([P, N], U32, name=f"kq{b}", align_bytes=64) for b in range(B)]
+        ks = [keep.tile([P, N], U8, name=f"ks{b}", align_bytes=64) for b in range(B)]
+        vq = [keep.tile([P, 2, 2 * P], U32, name=f"vq{b}", align_bytes=64) for b in range(B)]
+        vs = [keep.tile([P, 2, 2 * P], U8, name=f"vs{b}", align_bytes=64) for b in range(B)]
+
+        def cast(i):
+            u, c0, w, wv = CHUNKS[i]
+            nc.vector.tensor_copy(
+                out=words[u][:, c0 : c0 + wv, :], in_=raw[i][:, :, 0:wv].rearrange("p e n -> p n e")
+            )
+            nc.scalar.activation(
+                out=words[u][:, c0 + wv : c0 + w, :], in_=raw[i][:, :, wv:w].rearrange("p e n -> p n e"), func=ACT.Copy
+            )
+
+        def gather(b, u):
+            nc.vector.tensor_copy(
+                out=keys[b][:].bitcast(U32).rearrange("p (n u) -> p n u", u=2)[:, :, u],
+                in_=words[u][:].rearrange("p n e -> p (n e)").bitcast(U32).indirect(
+                    offsets[:, b * (N // 16) : (b + 1) * (N // 16)]
+                ),
+            )
+
+        def values(b, u):
+            turned = psum.tile([P, 4, 2 * P], BF16, name="turned", bufs=2)
+            rows = keys[b][:].rearrange("p (s j f) -> p j f s", j=4, f=4)
+            for j in range(4):
+                for e in range(2):
+                    nc.tensor.transpose(turned[:, j, e * P : (e + 1) * P], rows[:, j, 2 * u + e, :], ident_b[:])
+            val = stage.tile([P, 2 * P, 4], BF16, name="val", align_bytes=64)
+            nc.scalar.copy(out=val[:], in_=turned[:].rearrange("p j c -> p c j"))
+            return val
+
+        def quant_values(b, u, val):
+            nc.vector.quantize_mx(
+                out=vq[b][:, u, :].bitcast(FP8X4), scales=vs[b][:, u, :], in_=val[:].rearrange("p c j -> p (c j)")
+            )
+
+        def exp_weights(b):
+            pb = keep.tile([P, 4, P], F32, name=f"p{b}")
+            tb = keep.tile([P, 1], F32, name=f"total{b}")
+            nc.scalar.activation(
+                out=pb[:].rearrange("q j s -> q (j s)"),
+                in_=a[b][:].rearrange("q j s -> q (j s)"),
+                func=ACT.Exp,
+                bias=neg_m[b][:],
+                scale=1.0,
+                accum_out=tb[:],
+            )
+            p.append(pb)
+            total.append(tb)
+
+        def token_scales(b):
+            tok = keep.tile([P, N], F32, name=f"tok{b}")
+            nc.vector.tensor_copy(out=tok[:], in_=ts_sb[:].indirect(offsets[:, b * (N // 16) : (b + 1) * (N // 16)]))
+            toks.append(tok)
+
+        def scale_and_max(b):
+            ab = keep.tile([P, 4, P], F32, name=f"a{b}")
+            nc.vector.tensor_tensor(
+                out=ab[:].rearrange("q j s -> q s j"),
+                in0=scores[b][:].rearrange("q (s j) -> q s j", j=4),
+                in1=toks[b][:].rearrange("q (s j) -> q s j", j=4),
+                op=ALU.mult,
+            )
+            nm = keep.tile([P, 1], F32, name=f"nm{b}")
+            nc.vector.tensor_reduce(
+                out=nm[:], in_=ab[:].rearrange("q j s -> q (j s)"), axis=mybir.AxisListType.X, op=ALU.max, negate=True
+            )
+            a.append(ab)
+            neg_m.append(nm)
+
+        def token_columns(b):
+            tt = psum.tile([P, 4, P], F32, name="tt", tag="pt", bufs=2)
+            for j in range(4):
+                nc.tensor.transpose(tt[:, j, :], toks[b][:].rearrange("q (s j) -> q j s", j=4)[:, j, :], ident_f[:])
+            tc_b = keep.tile([P, 4], F32, name=f"tcol{b}")
+            nc.scalar.copy(out=tc_b[:], in_=tt[:, :, 0])
+            tcol.append(tc_b)
+
+        def turn_weights(b):
+            pt = psum.tile([P, 4, P], F32, name="pt", tag="pt", bufs=2)
+            for j in range(4):
+                nc.tensor.transpose(pt[:, j, :], p[b][:, j, :], ident_f[:])
+            pts.append(pt)
+
+        def weights(b):
+            wt = keep.tile([P, NQ, 4], BF16, name=f"w{b}", align_bytes=64)
+            nc.vector.tensor_tensor(
+                out=wt[:],
+                in0=pts[b][:].rearrange("s j q -> s q j"),
+                in1=tcol[b][:].unsqueeze(1).to_broadcast([P, NQ, 4]),
+                op=ALU.mult,
+            )
+            wq = keep.tile([P, NQ], U32, name=f"wq{b}", align_bytes=64)
+            ws = keep.tile([P, NQ], U8, name=f"ws{b}", align_bytes=64)
+            nc.vector.quantize_mx(out=wq[:].bitcast(FP8X4), scales=ws[:], in_=wt[:].rearrange("s q j -> s (q j)"))
+            wqs.append((wq, ws))
+
+        def mix(b):
+            wq, ws = wqs[b]
+            y = psum.tile([P, DV], F32, name="y", bufs=2)
+            for u in range(2):
+                nc.tensor.matmul_mx(
+                    out=y[:, u * 2 * P : (u + 1) * 2 * P],
+                    lhsT=wq[:].bitcast(FP8X4),
+                    lhsT_scale=ws[:],
+                    rhs=vq[b][:, u, :].bitcast(FP8X4),
+                    rhs_scale=vs[b][:, u, :],
+                    start=True,
+                    stop=True,
+                )
+            ys.append(y)
+
+        def finish(b):
+            inv = keep.tile([P, 1], F32, name=f"inv{b}")
+            nc.vector.reciprocal(out=inv[:], in_=total[b][:])
+            o = keep.tile([P, DV], F32, name=f"o{b}")
+            nc.vector.scalar_tensor_tensor(
+                out=o[:].rearrange("q (p f) -> q p f", f=4),
+                in0=ys[b][:].rearrange("q (f p) -> q p f", f=4),
+                scalar=inv[:],
+                in1=ch_sb[:].rearrange("q (p f) -> q p f", f=4),
+                op0=ALU.mult,
+                op1=ALU.mult,
+            )
+            nc.sync.dma_start(out=out[b], in_=o[:])
+
+        def quant_keys(b):
+            nc.vector.quantize_mx(out=kq[b][:].bitcast(FP8X4), scales=ks[b][:], in_=keys[b][:])
+
+        def score(b):
+            sc = psum.tile([P, N], F32, name="sc", bufs=2)
+            nc.tensor.matmul_mx(
+                out=sc[:],
+                lhsT=qq[:, b * NQ : (b + 1) * NQ].bitcast(FP8X4),
+                lhsT_scale=qs[:, b * NQ : (b + 1) * NQ],
+                rhs=kq[b][:].bitcast(FP8X4),
+                rhs_scale=ks[b][:],
+                start=True,
+                stop=True,
+            )
+            scores.append(sc)
+
+        a, neg_m, p, total, tcol, toks, scores, pts, wqs, ys = [], [], [], [], [], [], [], [], [], []
+        cast(0)
+        cast(1)
+        gather(0, 0)
+        gather(1, 0)
+        cast(2)
+        val00 = values(0, 0)
+        val10 = values(1, 0)
+        cast(3)
+        cast(4)
+        quant_values(0, 0, val00)
+        quant_values(1, 0, val10)
+        cast(5)
+
+        gather(0, 1)
+        q_sb = keep.tile([P, B, NQ, PACK], BF16, name="q_sb", align_bytes=64)
+        for b in range(B):
+            nc.scalar.activation(out=q_sb[:, b], in_=q_raw[:, b].rearrange("p t q -> p q t"), func=ACT.Copy)
+        qq = keep.tile([P, B * NQ], U32, name="qq", align_bytes=64)
+        qs = keep.tile([P, B * NQ], U8, name="qs", align_bytes=64)
+        quant_keys(0)
+        gather(1, 1)
+        nc.vector.quantize_mx(
+            out=qq[:].bitcast(FP8X4), scales=qs[:], in_=q_sb[:].rearrange("p b q t -> p (b q t)")
+        )
+        score(0)
+        quant_keys(1)
+        score(1)
+        token_scales(0)
+        scale_and_max(0)
+        exp_weights(0)
+        token_scales(1)
+        scale_and_max(1)
+        exp_weights(1)
+        token_columns(0)
+        turn_weights(0)
+        val01 = values(0, 1)
+        quant_values(0, 1, val01)
+        weights(0)
+        token_columns(1)
+        turn_weights(1)
+        mix(0)
+        val11 = values(1, 1)
+        quant_values(1, 1, val11)
+        weights(1)
+        mix(1)
+        finish(0)
+        finish(1)

@@ -17,14 +17,14 @@ FP8X4 = mybir.dt.float8_e4m3fn_x4
 ACT = mybir.ActivationFunctionType
 ALU = mybir.AluOpType
 
-CHUNKS = [(0, 0, 1024, 512), (0, 1024, 1024, 512), (1, 0, 1024, 512), (1, 1024, 512, 256), (1, 1536, 256, 128), (1, 1792, 256, 160)]
+CHUNKS = [(0, 0, 512, 344), (0, 512, 512, 344), (0, 1024, 512, 344), (0, 1536, 512, 344), (1, 0, 512, 0), (1, 512, 512, 0), (1, 1024, 512, 512), (1, 1536, 512, 512)]
 
 
 def tile_attend_mla_kernel(tc, qT, cT, ts, ch, offs, out):
     nc = tc.nc
     with ExitStack() as ctx:
         keep = ctx.enter_context(tc.tile_pool(name="keep", bufs=1))
-        stage = ctx.enter_context(tc.tile_pool(name="stage", bufs=2))
+        stage = ctx.enter_context(tc.tile_pool(name="stage", bufs=4))
         psum = ctx.enter_context(tc.psum_pool(name="psum", bufs=1))
 
         offsets = keep.tile([P, B * N // 16], U16, name="offsets")
@@ -53,6 +53,7 @@ def tile_attend_mla_kernel(tc, qT, cT, ts, ch, offs, out):
 
         words = [keep.tile([P, T, 2], BF16, name=f"words{u}") for u in range(2)]
         keys = [keep.tile([P, N * PACK], BF16, name=f"keys{b}", align_bytes=64) for b in range(B)]
+        picked = [keep.tile([P, 2, 4, P, 2], BF16, name=f"picked{b}") for b in range(B)]
         kq = [keep.tile([P, N], U32, name=f"kq{b}", align_bytes=64) for b in range(B)]
         ks = [keep.tile([P, N], U8, name=f"ks{b}", align_bytes=64) for b in range(B)]
         vq = [keep.tile([P, 2, 2 * P], U32, name=f"vq{b}", align_bytes=64) for b in range(B)]
@@ -60,16 +61,20 @@ def tile_attend_mla_kernel(tc, qT, cT, ts, ch, offs, out):
 
         def cast(i):
             u, c0, w, wv = CHUNKS[i]
-            nc.vector.tensor_copy(
-                out=words[u][:, c0 : c0 + wv, :], in_=raw[i][:, :, 0:wv].rearrange("p e n -> p n e")
-            )
-            nc.scalar.activation(
-                out=words[u][:, c0 + wv : c0 + w, :], in_=raw[i][:, :, wv:w].rearrange("p e n -> p n e"), func=ACT.Copy
-            )
+            if wv > 0:
+                nc.vector.tensor_copy(
+                    out=words[u][:, c0 : c0 + wv, :], in_=raw[i][:, :, 0:wv].rearrange("p e n -> p n e")
+                )
+            if wv < w:
+                nc.scalar.activation(
+                    out=words[u][:, c0 + wv : c0 + w, :],
+                    in_=raw[i][:, :, wv:w].rearrange("p e n -> p n e"),
+                    func=ACT.Copy,
+                )
 
         def gather(b, u):
             nc.vector.tensor_copy(
-                out=keys[b][:].bitcast(U32).rearrange("p (n u) -> p n u", u=2)[:, :, u],
+                out=picked[b][:, u].rearrange("p j s e -> p (j s e)").bitcast(U32).rearrange("p (j s) -> p s j", j=4),
                 in_=words[u][:].rearrange("p n e -> p (n e)").bitcast(U32).indirect(
                     offsets[:, b * (N // 16) : (b + 1) * (N // 16)]
                 ),
@@ -77,11 +82,10 @@ def tile_attend_mla_kernel(tc, qT, cT, ts, ch, offs, out):
 
         def values(b, u):
             turned = psum.tile([P, 4, 2 * P], BF16, name="turned", bufs=2)
-            rows = keys[b][:].rearrange("p (s j f) -> p j f s", j=4, f=4)
             for j in range(4):
                 for e in range(2):
-                    nc.tensor.transpose(turned[:, j, e * P : (e + 1) * P], rows[:, j, 2 * u + e, :], ident_b[:])
-            val = stage.tile([P, 2 * P, 4], BF16, name="val", align_bytes=64)
+                    nc.tensor.transpose(turned[:, j, e * P : (e + 1) * P], picked[b][:, u, j, :, e], ident_b[:])
+            val = stage.tile([P, 2 * P, 4], BF16, name="val", align_bytes=64, bufs=4)
             nc.scalar.copy(out=val[:], in_=turned[:].rearrange("p j c -> p c j"))
             return val
 
@@ -109,19 +113,21 @@ def tile_attend_mla_kernel(tc, qT, cT, ts, ch, offs, out):
             nc.vector.tensor_copy(out=tok[:], in_=ts_sb[:].indirect(offsets[:, b * (N // 16) : (b + 1) * (N // 16)]))
             toks.append(tok)
 
-        def scale_and_max(b):
+        def scale_scores(b):
             ab = keep.tile([P, 4, P], F32, name=f"a{b}")
             nc.vector.tensor_tensor(
                 out=ab[:].rearrange("q j s -> q s j"),
-                in0=scores[b][:].rearrange("q (s j) -> q s j", j=4),
+                in0=scores[b][:].rearrange("q (j s) -> q s j", j=4),
                 in1=toks[b][:].rearrange("q (s j) -> q s j", j=4),
                 op=ALU.mult,
             )
+            a.append(ab)
+
+        def row_max(b):
             nm = keep.tile([P, 1], F32, name=f"nm{b}")
             nc.vector.tensor_reduce(
-                out=nm[:], in_=ab[:].rearrange("q j s -> q (j s)"), axis=mybir.AxisListType.X, op=ALU.max, negate=True
+                out=nm[:], in_=a[b][:].rearrange("q j s -> q (j s)"), axis=mybir.AxisListType.X, op=ALU.max, negate=True
             )
-            a.append(ab)
             neg_m.append(nm)
 
         def token_columns(b):
@@ -146,6 +152,10 @@ def tile_attend_mla_kernel(tc, qT, cT, ts, ch, offs, out):
                 in1=tcol[b][:].unsqueeze(1).to_broadcast([P, NQ, 4]),
                 op=ALU.mult,
             )
+            wts.append(wt)
+
+        def quant_weights(b):
+            wt = wts[b]
             wq = keep.tile([P, NQ], U32, name=f"wq{b}", align_bytes=64)
             ws = keep.tile([P, NQ], U8, name=f"ws{b}", align_bytes=64)
             nc.vector.quantize_mx(out=wq[:].bitcast(FP8X4), scales=ws[:], in_=wt[:].rearrange("s q j -> s (q j)"))
@@ -166,19 +176,34 @@ def tile_attend_mla_kernel(tc, qT, cT, ts, ch, offs, out):
                 )
             ys.append(y)
 
-        def finish(b):
+        def invert(b):
             inv = keep.tile([P, 1], F32, name=f"inv{b}")
             nc.vector.reciprocal(out=inv[:], in_=total[b][:])
+            invs.append(inv)
+
+        def finish(b):
             o = keep.tile([P, DV], F32, name=f"o{b}")
             nc.vector.scalar_tensor_tensor(
                 out=o[:].rearrange("q (p f) -> q p f", f=4),
                 in0=ys[b][:].rearrange("q (f p) -> q p f", f=4),
-                scalar=inv[:],
+                scalar=invs[b][:],
                 in1=ch_sb[:].rearrange("q (p f) -> q p f", f=4),
                 op0=ALU.mult,
                 op1=ALU.mult,
             )
             nc.sync.dma_start(out=out[b], in_=o[:])
+
+        def interleave_keys(b):
+            if b == 0:
+                nc.vector.tensor_copy(
+                    out=keys[b][:].bitcast(F32).rearrange("p (n u) -> p n u", u=2),
+                    in_=picked[b][:].rearrange("p u j s e -> p (u j s e)").bitcast(F32).rearrange("p (u n) -> p n u", u=2),
+                )
+            else:
+                nc.scalar.copy(
+                    out=keys[b][:].rearrange("p (n u e) -> p n u e", u=2, e=2),
+                    in_=picked[b][:].rearrange("p u j s e -> p (j s) u e"),
+                )
 
         def quant_keys(b):
             nc.vector.quantize_mx(out=kq[b][:].bitcast(FP8X4), scales=ks[b][:], in_=keys[b][:])
@@ -196,51 +221,50 @@ def tile_attend_mla_kernel(tc, qT, cT, ts, ch, offs, out):
             )
             scores.append(sc)
 
-        a, neg_m, p, total, tcol, toks, scores, pts, wqs, ys = [], [], [], [], [], [], [], [], [], []
-        cast(0)
-        cast(1)
+        a, neg_m, p, total, tcol, toks, scores, pts, wts, wqs, ys, invs = [], [], [], [], [], [], [], [], [], [], [], []
+        for i in range(8):
+            cast(i)
         gather(0, 0)
         gather(1, 0)
-        cast(2)
-        val00 = values(0, 0)
-        val10 = values(1, 0)
-        cast(3)
-        cast(4)
-        quant_values(0, 0, val00)
-        quant_values(1, 0, val10)
-        cast(5)
-
         gather(0, 1)
+        gather(1, 1)
         q_sb = keep.tile([P, B, NQ, PACK], BF16, name="q_sb", align_bytes=64)
         for b in range(B):
             nc.scalar.activation(out=q_sb[:, b], in_=q_raw[:, b].rearrange("p t q -> p q t"), func=ACT.Copy)
         qq = keep.tile([P, B * NQ], U32, name="qq", align_bytes=64)
         qs = keep.tile([P, B * NQ], U8, name="qs", align_bytes=64)
-        quant_keys(0)
-        gather(1, 1)
+        interleave_keys(0)
+        interleave_keys(1)
         nc.vector.quantize_mx(
             out=qq[:].bitcast(FP8X4), scales=qs[:], in_=q_sb[:].rearrange("p b q t -> p (b q t)")
         )
+        quant_keys(0)
         score(0)
+        token_scales(0)
         quant_keys(1)
         score(1)
-        token_scales(0)
-        scale_and_max(0)
-        exp_weights(0)
+        scale_scores(0)
         token_scales(1)
-        scale_and_max(1)
+        row_max(0)
+        exp_weights(0)
+        scale_scores(1)
+        row_max(1)
         exp_weights(1)
+        vals = [[values(b, u) for u in range(2)] for b in range(B)]
         token_columns(0)
         turn_weights(0)
-        val01 = values(0, 1)
-        quant_values(0, 1, val01)
         weights(0)
+        quant_weights(0)
         token_columns(1)
         turn_weights(1)
-        mix(0)
-        val11 = values(1, 1)
-        quant_values(1, 1, val11)
         weights(1)
+        quant_weights(1)
+        for b in range(B):
+            for u in range(2):
+                quant_values(b, u, vals[b][u])
+        invert(0)
+        invert(1)
+        mix(0)
         mix(1)
         finish(0)
         finish(1)

@@ -17,18 +17,18 @@ FP8X4 = mybir.dt.float8_e4m3fn_x4
 ACT = mybir.ActivationFunctionType
 ALU = mybir.AluOpType
 
-CHUNKS = [(0, 0, 512, 344), (0, 512, 512, 344), (0, 1024, 512, 344), (0, 1536, 512, 344), (1, 0, 512, 0), (1, 512, 512, 0), (1, 1024, 512, 512), (1, 1536, 512, 512)]
+CHUNKS = [(0, 0, 1024, 688), (0, 1024, 1024, 688), (1, 0, 512, 0), (1, 512, 1024, 1024), (1, 1536, 512, 512)]
 
 
 def tile_attend_mla_kernel(tc, qT, cT, ts, ch, offs, out):
     nc = tc.nc
     with ExitStack() as ctx:
         keep = ctx.enter_context(tc.tile_pool(name="keep", bufs=1))
-        stage = ctx.enter_context(tc.tile_pool(name="stage", bufs=4))
         psum = ctx.enter_context(tc.psum_pool(name="psum", bufs=1))
 
         offsets = keep.tile([P, B * N // 16], U16, name="offsets")
         nc.sync.dma_start(offsets[:], offs)
+        lists = [offsets[:, b * (N // 16) : (b + 1) * (N // 16)] for b in range(B)]
         pool_rows = cT.rearrange("(p t) n -> p t n", t=PACK)
         raw = []
         for i, (u, c0, w, wv) in enumerate(CHUNKS):
@@ -52,136 +52,177 @@ def tile_attend_mla_kernel(tc, qT, cT, ts, ch, offs, out):
         nc.scalar.activation(out=warm2[:], in_=warm[:], func=ACT.Exp)
 
         words = [keep.tile([P, T, 2], BF16, name=f"words{u}") for u in range(2)]
-        keys = [keep.tile([P, N * PACK], BF16, name=f"keys{b}", align_bytes=64) for b in range(B)]
         picked = [keep.tile([P, 2, 4, P, 2], BF16, name=f"picked{b}") for b in range(B)]
+        keys = [keep.tile([P, N, 2, 2], BF16, name=f"keys{b}", align_bytes=64) for b in range(B)]
         kq = [keep.tile([P, N], U32, name=f"kq{b}", align_bytes=64) for b in range(B)]
         ks = [keep.tile([P, N], U8, name=f"ks{b}", align_bytes=64) for b in range(B)]
-        vq = [keep.tile([P, 2, 2 * P], U32, name=f"vq{b}", align_bytes=64) for b in range(B)]
-        vs = [keep.tile([P, 2, 2 * P], U8, name=f"vs{b}", align_bytes=64) for b in range(B)]
+        vals = [keep.tile([P, DV, 4], BF16, name=f"vals{b}", align_bytes=64) for b in range(B)]
+        q_sb = keep.tile([P, B, NQ, PACK], BF16, name="q_sb", align_bytes=64)
+        qq = keep.tile([P, B * NQ], U32, name="qq", align_bytes=64)
+        qs = keep.tile([P, B * NQ], U8, name="qs", align_bytes=64)
+        toks = keep.tile([P, B, N], F32, name="toks", tag="toks", align_bytes=64)
+        turned, scores, tts, tcol, a, neg_m, p, total, pts, wts, wqs, invs, ys, vqs = ({} for i in range(14))
 
-        def cast(i):
+        def cv(i):
             u, c0, w, wv = CHUNKS[i]
-            if wv > 0:
-                nc.vector.tensor_copy(
-                    out=words[u][:, c0 : c0 + wv, :], in_=raw[i][:, :, 0:wv].rearrange("p e n -> p n e")
-                )
-            if wv < w:
-                nc.scalar.activation(
-                    out=words[u][:, c0 + wv : c0 + w, :],
-                    in_=raw[i][:, :, wv:w].rearrange("p e n -> p n e"),
-                    func=ACT.Copy,
-                )
+            nc.vector.tensor_copy(
+                out=words[u][:, c0 : c0 + wv, :], in_=raw[i][:, :, 0:wv].rearrange("p e n -> p n e")
+            )
 
-        def gather(b, u):
+        def cs(i):
+            u, c0, w, wv = CHUNKS[i]
+            nc.scalar.activation(
+                out=words[u][:, c0 + wv : c0 + w, :],
+                in_=raw[i][:, :, wv:w].rearrange("p e n -> p n e"),
+                func=ACT.Copy,
+            )
+
+        def g(b, u):
             nc.vector.tensor_copy(
                 out=picked[b][:, u].rearrange("p j s e -> p (j s e)").bitcast(U32).rearrange("p (j s) -> p s j", j=4),
-                in_=words[u][:].rearrange("p n e -> p (n e)").bitcast(U32).indirect(
-                    offsets[:, b * (N // 16) : (b + 1) * (N // 16)]
-                ),
+                in_=words[u][:].rearrange("p n e -> p (n e)").bitcast(U32).indirect(lists[b]),
             )
 
-        def values(b, u):
-            turned = psum.tile([P, 4, 2 * P], BF16, name="turned", bufs=2)
+        def tv(b, u):
+            t = psum.tile([P, 4, 2 * P], BF16, name="turned", bufs=4)
             for j in range(4):
                 for e in range(2):
-                    nc.tensor.transpose(turned[:, j, e * P : (e + 1) * P], picked[b][:, u, j, :, e], ident_b[:])
-            val = stage.tile([P, 2 * P, 4], BF16, name="val", align_bytes=64, bufs=4)
-            nc.scalar.copy(out=val[:], in_=turned[:].rearrange("p j c -> p c j"))
-            return val
+                    nc.tensor.transpose(t[:, j, e * P : (e + 1) * P], picked[b][:, u, j, :, e], ident_b[:])
+            turned[b, u] = t
 
-        def quant_values(b, u, val):
-            nc.vector.quantize_mx(
-                out=vq[b][:, u, :].bitcast(FP8X4), scales=vs[b][:, u, :], in_=val[:].rearrange("p c j -> p (c j)")
+        def vc(b, u):
+            nc.scalar.copy(
+                out=vals[b][:, u * 2 * P : (u + 1) * 2 * P, :], in_=turned[b, u][:].rearrange("p j c -> p c j")
             )
 
-        def exp_weights(b):
-            pb = keep.tile([P, 4, P], F32, name=f"p{b}")
-            tb = keep.tile([P, 1], F32, name=f"total{b}")
+        def qv(b):
+            if "vq" not in vqs:
+                vqs["vq"] = keep.tile([P, B, DV], U32, name="vq", tag="toks", align_bytes=64)
+                vqs["vs"] = keep.tile([P, B, DV], U8, name="vs", align_bytes=64)
+            nc.vector.quantize_mx(
+                out=vqs["vq"][:, b, :].bitcast(FP8X4),
+                scales=vqs["vs"][:, b, :],
+                in_=vals[b][:].rearrange("p c j -> p (c j)"),
+            )
+
+        def qc(b):
+            nc.scalar.activation(out=q_sb[:, b], in_=q_raw[:, b].rearrange("p t q -> p q t"), func=ACT.Copy)
+
+        def qQ():
+            nc.vector.quantize_mx(
+                out=qq[:].bitcast(FP8X4), scales=qs[:], in_=q_sb[:].rearrange("p b q t -> p (b q t)")
+            )
+
+        def ilv(b):
+            if b == 0:
+                nc.vector.tensor_copy(
+                    out=keys[b][:].rearrange("p n u e -> p (n u e)").bitcast(F32).rearrange("p (n u) -> p n u", u=2),
+                    in_=picked[b][:].rearrange("p u j s e -> p (u j s e)").bitcast(F32).rearrange("p (u n) -> p n u", u=2),
+                )
+            else:
+                nc.scalar.copy(out=keys[b][:], in_=picked[b][:].rearrange("p u j s e -> p (j s) u e"))
+
+        def qK(b):
+            nc.vector.quantize_mx(
+                out=kq[b][:].bitcast(FP8X4), scales=ks[b][:], in_=keys[b][:].rearrange("p n u e -> p (n u e)")
+            )
+
+        def mm(b):
+            sc = psum.tile([P, N], F32, name="sc", tag="sc", bufs=2)
+            nc.tensor.matmul_mx(
+                out=sc[:],
+                lhsT=qq[:, b * NQ : (b + 1) * NQ].bitcast(FP8X4),
+                lhsT_scale=qs[:, b * NQ : (b + 1) * NQ],
+                rhs=kq[b][:].bitcast(FP8X4),
+                rhs_scale=ks[b][:],
+                start=True,
+                stop=True,
+            )
+            scores[b] = sc
+
+        def tok(b):
+            nc.vector.tensor_copy(out=toks[:, b, :], in_=ts_sb[:].indirect(lists[b]))
+
+        def tt(b):
+            t = psum.tile([P, 4, P], F32, name="tt", tag="pt", bufs=2)
+            for j in range(4):
+                nc.tensor.transpose(t[:, j, :], toks[:, b, :].rearrange("q (s j) -> q j s", j=4)[:, j, :], ident_f[:])
+            tts[b] = t
+
+        def tcl(b):
+            tcol[b] = keep.tile([P, 4], F32, name=f"tcol{b}")
+            nc.scalar.copy(out=tcol[b][:], in_=tts[b][:, :, 0])
+
+        def sca(b):
+            a[b] = keep.tile([P, 4, P], F32, name=f"a{b}")
+            nc.vector.tensor_tensor(
+                out=a[b][:].rearrange("q j s -> q s j"),
+                in0=scores[b][:].rearrange("q (j s) -> q s j", j=4),
+                in1=toks[:, b, :].rearrange("q (s j) -> q s j", j=4),
+                op=ALU.mult,
+            )
+
+        def mx(b):
+            neg_m[b] = keep.tile([P, 1], F32, name=f"nm{b}")
+            nc.vector.tensor_reduce(
+                out=neg_m[b][:],
+                in_=a[b][:].rearrange("q j s -> q (j s)"),
+                axis=mybir.AxisListType.X,
+                op=ALU.max,
+                negate=True,
+            )
+
+        def ex(b):
+            p[b] = keep.tile([P, 4, P], F32, name=f"p{b}")
+            total[b] = keep.tile([P, 1], F32, name=f"total{b}")
             nc.scalar.activation(
-                out=pb[:].rearrange("q j s -> q (j s)"),
+                out=p[b][:].rearrange("q j s -> q (j s)"),
                 in_=a[b][:].rearrange("q j s -> q (j s)"),
                 func=ACT.Exp,
                 bias=neg_m[b][:],
                 scale=1.0,
-                accum_out=tb[:],
+                accum_out=total[b][:],
             )
-            p.append(pb)
-            total.append(tb)
 
-        def token_scales(b):
-            tok = keep.tile([P, N], F32, name=f"tok{b}")
-            nc.vector.tensor_copy(out=tok[:], in_=ts_sb[:].indirect(offsets[:, b * (N // 16) : (b + 1) * (N // 16)]))
-            toks.append(tok)
-
-        def scale_scores(b):
-            ab = keep.tile([P, 4, P], F32, name=f"a{b}")
-            nc.vector.tensor_tensor(
-                out=ab[:].rearrange("q j s -> q s j"),
-                in0=scores[b][:].rearrange("q (j s) -> q s j", j=4),
-                in1=toks[b][:].rearrange("q (s j) -> q s j", j=4),
-                op=ALU.mult,
-            )
-            a.append(ab)
-
-        def row_max(b):
-            nm = keep.tile([P, 1], F32, name=f"nm{b}")
-            nc.vector.tensor_reduce(
-                out=nm[:], in_=a[b][:].rearrange("q j s -> q (j s)"), axis=mybir.AxisListType.X, op=ALU.max, negate=True
-            )
-            neg_m.append(nm)
-
-        def token_columns(b):
-            tt = psum.tile([P, 4, P], F32, name="tt", tag="pt", bufs=2)
+        def pt(b):
+            t = psum.tile([P, 4, P], F32, name="pt", tag="pt", bufs=2)
             for j in range(4):
-                nc.tensor.transpose(tt[:, j, :], toks[b][:].rearrange("q (s j) -> q j s", j=4)[:, j, :], ident_f[:])
-            tc_b = keep.tile([P, 4], F32, name=f"tcol{b}")
-            nc.scalar.copy(out=tc_b[:], in_=tt[:, :, 0])
-            tcol.append(tc_b)
+                nc.tensor.transpose(t[:, j, :], p[b][:, j, :], ident_f[:])
+            pts[b] = t
 
-        def turn_weights(b):
-            pt = psum.tile([P, 4, P], F32, name="pt", tag="pt", bufs=2)
-            for j in range(4):
-                nc.tensor.transpose(pt[:, j, :], p[b][:, j, :], ident_f[:])
-            pts.append(pt)
-
-        def weights(b):
-            wt = keep.tile([P, NQ, 4], BF16, name=f"w{b}", align_bytes=64)
+        def w(b):
+            wts[b] = keep.tile([P, NQ, 4], BF16, name=f"w{b}", align_bytes=64)
             nc.vector.tensor_tensor(
-                out=wt[:],
+                out=wts[b][:],
                 in0=pts[b][:].rearrange("s j q -> s q j"),
                 in1=tcol[b][:].unsqueeze(1).to_broadcast([P, NQ, 4]),
                 op=ALU.mult,
             )
-            wts.append(wt)
 
-        def quant_weights(b):
-            wt = wts[b]
+        def qw(b):
             wq = keep.tile([P, NQ], U32, name=f"wq{b}", align_bytes=64)
             ws = keep.tile([P, NQ], U8, name=f"ws{b}", align_bytes=64)
-            nc.vector.quantize_mx(out=wq[:].bitcast(FP8X4), scales=ws[:], in_=wt[:].rearrange("s q j -> s (q j)"))
-            wqs.append((wq, ws))
+            nc.vector.quantize_mx(out=wq[:].bitcast(FP8X4), scales=ws[:], in_=wts[b][:].rearrange("s q j -> s (q j)"))
+            wqs[b] = (wq, ws)
+
+        def rec(b):
+            invs[b] = keep.tile([P, 1], F32, name=f"inv{b}")
+            nc.vector.reciprocal(out=invs[b][:], in_=total[b][:])
 
         def mix(b):
             wq, ws = wqs[b]
-            y = psum.tile([P, DV], F32, name="y", bufs=2)
-            for u in range(2):
-                nc.tensor.matmul_mx(
-                    out=y[:, u * 2 * P : (u + 1) * 2 * P],
-                    lhsT=wq[:].bitcast(FP8X4),
-                    lhsT_scale=ws[:],
-                    rhs=vq[b][:, u, :].bitcast(FP8X4),
-                    rhs_scale=vs[b][:, u, :],
-                    start=True,
-                    stop=True,
-                )
-            ys.append(y)
+            ys[b] = psum.tile([P, DV], F32, name="y", tag="sc", bufs=2)
+            nc.tensor.matmul_mx(
+                out=ys[b][:],
+                lhsT=wq[:].bitcast(FP8X4),
+                lhsT_scale=ws[:],
+                rhs=vqs["vq"][:, b, :].bitcast(FP8X4),
+                rhs_scale=vqs["vs"][:, b, :],
+                start=True,
+                stop=True,
+            )
 
-        def invert(b):
-            inv = keep.tile([P, 1], F32, name=f"inv{b}")
-            nc.vector.reciprocal(out=inv[:], in_=total[b][:])
-            invs.append(inv)
-
-        def finish(b):
+        def fin(b):
             o = keep.tile([P, DV], F32, name=f"o{b}")
             nc.vector.scalar_tensor_tensor(
                 out=o[:].rearrange("q (p f) -> q p f", f=4),
@@ -193,78 +234,57 @@ def tile_attend_mla_kernel(tc, qT, cT, ts, ch, offs, out):
             )
             nc.sync.dma_start(out=out[b], in_=o[:])
 
-        def interleave_keys(b):
-            if b == 0:
-                nc.vector.tensor_copy(
-                    out=keys[b][:].bitcast(F32).rearrange("p (n u) -> p n u", u=2),
-                    in_=picked[b][:].rearrange("p u j s e -> p (u j s e)").bitcast(F32).rearrange("p (u n) -> p n u", u=2),
-                )
-            else:
-                nc.scalar.copy(
-                    out=keys[b][:].rearrange("p (n u e) -> p n u e", u=2, e=2),
-                    in_=picked[b][:].rearrange("p u j s e -> p (j s) u e"),
-                )
-
-        def quant_keys(b):
-            nc.vector.quantize_mx(out=kq[b][:].bitcast(FP8X4), scales=ks[b][:], in_=keys[b][:])
-
-        def score(b):
-            sc = psum.tile([P, N], F32, name="sc", bufs=2)
-            nc.tensor.matmul_mx(
-                out=sc[:],
-                lhsT=qq[:, b * NQ : (b + 1) * NQ].bitcast(FP8X4),
-                lhsT_scale=qs[:, b * NQ : (b + 1) * NQ],
-                rhs=kq[b][:].bitcast(FP8X4),
-                rhs_scale=ks[b][:],
-                start=True,
-                stop=True,
-            )
-            scores.append(sc)
-
-        a, neg_m, p, total, tcol, toks, scores, pts, wts, wqs, ys, invs = [], [], [], [], [], [], [], [], [], [], [], []
-        for i in range(8):
-            cast(i)
-        gather(0, 0)
-        gather(1, 0)
-        gather(0, 1)
-        gather(1, 1)
-        q_sb = keep.tile([P, B, NQ, PACK], BF16, name="q_sb", align_bytes=64)
-        for b in range(B):
-            nc.scalar.activation(out=q_sb[:, b], in_=q_raw[:, b].rearrange("p t q -> p q t"), func=ACT.Copy)
-        qq = keep.tile([P, B * NQ], U32, name="qq", align_bytes=64)
-        qs = keep.tile([P, B * NQ], U8, name="qs", align_bytes=64)
-        interleave_keys(0)
-        interleave_keys(1)
-        nc.vector.quantize_mx(
-            out=qq[:].bitcast(FP8X4), scales=qs[:], in_=q_sb[:].rearrange("p b q t -> p (b q t)")
-        )
-        quant_keys(0)
-        score(0)
-        token_scales(0)
-        quant_keys(1)
-        score(1)
-        scale_scores(0)
-        token_scales(1)
-        row_max(0)
-        exp_weights(0)
-        scale_scores(1)
-        row_max(1)
-        exp_weights(1)
-        vals = [[values(b, u) for u in range(2)] for b in range(B)]
-        token_columns(0)
-        turn_weights(0)
-        weights(0)
-        quant_weights(0)
-        token_columns(1)
-        turn_weights(1)
-        weights(1)
-        quant_weights(1)
-        for b in range(B):
-            for u in range(2):
-                quant_values(b, u, vals[b][u])
-        invert(0)
-        invert(1)
+        cv(0)
+        cs(0)
+        cv(1)
+        cs(1)
+        g(0, 0)
+        cs(2)
+        g(1, 0)
+        tv(0, 0)
+        vc(0, 0)
+        cv(3)
+        tv(1, 0)
+        vc(1, 0)
+        cv(4)
+        qc(0)
+        qc(1)
+        g(0, 1)
+        g(1, 1)
+        ilv(1)
+        ilv(0)
+        tv(0, 1)
+        vc(0, 1)
+        tv(1, 1)
+        vc(1, 1)
+        qQ()
+        qK(0)
+        mm(0)
+        qK(1)
+        mm(1)
+        tok(0)
+        tt(0)
+        tcl(0)
+        tok(1)
+        tt(1)
+        tcl(1)
+        sca(0)
+        sca(1)
+        mx(0)
+        ex(0)
+        mx(1)
+        ex(1)
+        pt(0)
+        rec(0)
+        w(0)
+        pt(1)
+        qw(0)
+        qv(0)
         mix(0)
+        w(1)
+        rec(1)
+        qw(1)
+        qv(1)
         mix(1)
-        finish(0)
-        finish(1)
+        fin(0)
+        fin(1)

@@ -42,8 +42,6 @@ def tile_attend_mla_kernel(tc, qT, cT, ts, ch, offs, out):
         ch_sb = keep.tile([P, DV], F32, name="ch_sb")
         nc.sync.dma_start(out=ch_sb[:], in_=ch)
 
-        ident_b = keep.tile([P, P], BF16, name="ident_b")
-        make_identity(nc, ident_b[:])
         ident_f = keep.tile([P, P], F32, name="ident_f")
         make_identity(nc, ident_f[:])
         warm = keep.tile([P, 1], F32, name="warm")
@@ -52,7 +50,7 @@ def tile_attend_mla_kernel(tc, qT, cT, ts, ch, offs, out):
         nc.scalar.activation(out=warm2[:], in_=warm[:], func=ACT.Exp)
 
         words = [keep.tile([P, T, 2], BF16, name=f"words{u}") for u in range(2)]
-        picked = [keep.tile([P, 2, 4, P, 2], BF16, name=f"picked{b}") for b in range(B)]
+        picked = [keep.tile([P, 2, N, 2], BF16, name=f"picked{b}") for b in range(B)]
         keys = [keep.tile([P, N, 2, 2], BF16, name=f"keys{b}", align_bytes=64) for b in range(B)]
         kq = [keep.tile([P, N], U32, name=f"kq{b}", align_bytes=64) for b in range(B)]
         ks = [keep.tile([P, N], U8, name=f"ks{b}", align_bytes=64) for b in range(B)]
@@ -79,20 +77,21 @@ def tile_attend_mla_kernel(tc, qT, cT, ts, ch, offs, out):
 
         def g(b, u):
             nc.vector.tensor_copy(
-                out=picked[b][:, u].rearrange("p j s e -> p (j s e)").bitcast(U32).rearrange("p (j s) -> p s j", j=4),
+                out=picked[b][:, u].rearrange("p n e -> p (n e)").bitcast(U32),
                 in_=words[u][:].rearrange("p n e -> p (n e)").bitcast(U32).indirect(lists[b]),
             )
 
         def tv(b, u):
-            t = psum.tile([P, 4, 2 * P], BF16, name="turned", bufs=4)
+            t = psum.tile([P, 4, P], F32, name="turned", bufs=4)
+            pairs = picked[b][:, u].rearrange("p n e -> p (n e)").bitcast(F32).rearrange("p (s j) -> p j s", j=4)
             for j in range(4):
-                for e in range(2):
-                    nc.tensor.transpose(t[:, j, e * P : (e + 1) * P], picked[b][:, u, j, :, e], ident_b[:])
+                nc.tensor.transpose(t[:, j, :], pairs[:, j, :], ident_f[:])
             turned[b, u] = t
 
         def vc(b, u):
             nc.scalar.copy(
-                out=vals[b][:, u * 2 * P : (u + 1) * 2 * P, :], in_=turned[b, u][:].rearrange("p j c -> p c j")
+                out=vals[b][:, u * 2 * P : (u + 1) * 2 * P, :].rearrange("s (e p) j -> s e p j", e=2),
+                in_=turned[b, u][:].rearrange("s j p -> s (j p)").bitcast(BF16).rearrange("s (j p e) -> s e p j", j=4, e=2),
             )
 
         def qv(b):
@@ -117,10 +116,10 @@ def tile_attend_mla_kernel(tc, qT, cT, ts, ch, offs, out):
             if b == 0:
                 nc.vector.tensor_copy(
                     out=keys[b][:].rearrange("p n u e -> p (n u e)").bitcast(F32).rearrange("p (n u) -> p n u", u=2),
-                    in_=picked[b][:].rearrange("p u j s e -> p (u j s e)").bitcast(F32).rearrange("p (u n) -> p n u", u=2),
+                    in_=picked[b][:].rearrange("p u n e -> p (u n e)").bitcast(F32).rearrange("p (u n) -> p n u", u=2),
                 )
             else:
-                nc.scalar.copy(out=keys[b][:], in_=picked[b][:].rearrange("p u j s e -> p (j s) u e"))
+                nc.scalar.copy(out=keys[b][:], in_=picked[b][:].rearrange("p u n e -> p n u e"))
 
         def qK(b):
             nc.vector.quantize_mx(
@@ -154,19 +153,14 @@ def tile_attend_mla_kernel(tc, qT, cT, ts, ch, offs, out):
             nc.scalar.copy(out=tcol[b][:], in_=tts[b][:, :, 0])
 
         def sca(b):
-            a[b] = keep.tile([P, 4, P], F32, name=f"a{b}")
-            nc.vector.tensor_tensor(
-                out=a[b][:].rearrange("q j s -> q s j"),
-                in0=scores[b][:].rearrange("q (j s) -> q s j", j=4),
-                in1=toks[:, b, :].rearrange("q (s j) -> q s j", j=4),
-                op=ALU.mult,
-            )
+            a[b] = keep.tile([P, N], F32, name=f"a{b}")
+            nc.vector.tensor_tensor(out=a[b][:], in0=scores[b][:], in1=toks[:, b, :], op=ALU.mult)
 
         def mx(b):
             neg_m[b] = keep.tile([P, 1], F32, name=f"nm{b}")
             nc.vector.tensor_reduce(
                 out=neg_m[b][:],
-                in_=a[b][:].rearrange("q j s -> q (j s)"),
+                in_=a[b][:],
                 axis=mybir.AxisListType.X,
                 op=ALU.max,
                 negate=True,
@@ -176,8 +170,8 @@ def tile_attend_mla_kernel(tc, qT, cT, ts, ch, offs, out):
             p[b] = keep.tile([P, 4, P], F32, name=f"p{b}")
             total[b] = keep.tile([P, 1], F32, name=f"total{b}")
             nc.scalar.activation(
-                out=p[b][:].rearrange("q j s -> q (j s)"),
-                in_=a[b][:].rearrange("q j s -> q (j s)"),
+                out=p[b][:].rearrange("q j s -> q s j"),
+                in_=a[b][:].rearrange("q (s j) -> q s j", j=4),
                 func=ACT.Exp,
                 bias=neg_m[b][:],
                 scale=1.0,

from contextlib import ExitStack

import concourse.mybir as mybir
from concourse.masks import make_identity

B, N, T, D, DV, NQ = 2, 512, 2048, 512, 512, 128
P = 128
PACK = 4
FLOPS = 2 * B * NQ * N * (D + DV)

F32 = mybir.dt.float32
BF16 = mybir.dt.bfloat16
U32 = mybir.dt.uint32
U16 = mybir.dt.uint16
U8 = mybir.dt.uint8
FP8X4 = mybir.dt.float8_e4m3fn_x4
ACT = mybir.ActivationFunctionType
ALU = mybir.AluOpType

CHUNKS = [(0, 0, 1024, 688), (0, 1024, 1024, 688), (1, 0, 512, 0), (1, 512, 1024, 1024), (1, 1536, 512, 512)]


def tile_attend_mla_kernel(tc, qT, cT, ts, ch, offs, out):
    nc = tc.nc
    with ExitStack() as ctx:
        keep = ctx.enter_context(tc.tile_pool(name="keep", bufs=1))
        psum = ctx.enter_context(tc.psum_pool(name="psum", bufs=1))

        offsets = keep.tile([P, B * N // 16], U16, name="offsets")
        nc.sync.dma_start(offsets[:], offs)
        lists = [offsets[:, b * (N // 16) : (b + 1) * (N // 16)] for b in range(B)]
        pool_rows = cT.rearrange("(p t) n -> p t n", t=PACK)
        raw = []
        for i, (u, c0, w, wv) in enumerate(CHUNKS):
            r = keep.tile([P, 2, w], F32, name=f"raw{i}")
            nc.sync.dma_start(out=r[:], in_=pool_rows[:, 2 * u : 2 * u + 2, c0 : c0 + w])
            raw.append(r)
        q_raw = keep.tile([P, B, PACK, NQ], F32, name="q_raw")
        nc.sync.dma_start(out=q_raw[:], in_=qT.rearrange("b (p t) q -> p b t q", t=PACK))
        ts_sb = keep.tile([P, T], F32, name="ts_sb")
        nc.sync.dma_start(out=ts_sb[:], in_=ts)
        ch_sb = keep.tile([P, DV], F32, name="ch_sb")
        nc.sync.dma_start(out=ch_sb[:], in_=ch)

        ident_f = keep.tile([P, P], F32, name="ident_f")
        make_identity(nc, ident_f[:])
        warm = keep.tile([P, 1], F32, name="warm")
        nc.gpsimd.memset(warm[:], 0.0)
        warm2 = keep.tile([P, 1], F32, name="warm2")
        nc.scalar.activation(out=warm2[:], in_=warm[:], func=ACT.Exp)

        words = [keep.tile([P, T, 2], BF16, name=f"words{u}") for u in range(2)]
        picked = [keep.tile([P, 2, N, 2], BF16, name=f"picked{b}") for b in range(B)]
        keys = [keep.tile([P, N, 2, 2], BF16, name=f"keys{b}", align_bytes=64) for b in range(B)]
        kq = [keep.tile([P, N], U32, name=f"kq{b}", align_bytes=64) for b in range(B)]
        ks = [keep.tile([P, N], U8, name=f"ks{b}", align_bytes=64) for b in range(B)]
        vals = [keep.tile([P, DV, 4], BF16, name=f"vals{b}", align_bytes=64) for b in range(B)]
        q_sb = keep.tile([P, B, NQ, PACK], BF16, name="q_sb", align_bytes=64)
        qq = keep.tile([P, B * NQ], U32, name="qq", align_bytes=64)
        qs = keep.tile([P, B * NQ], U8, name="qs", align_bytes=64)
        toks = keep.tile([P, B, N], F32, name="toks", tag="toks", align_bytes=64)
        turned, scores, tts, tcol, a, neg_m, p, total, pts, wts, wqs, invs, ys, vqs = ({} for i in range(14))

        def cv(i):
            u, c0, w, wv = CHUNKS[i]
            nc.vector.tensor_copy(
                out=words[u][:, c0 : c0 + wv, :], in_=raw[i][:, :, 0:wv].rearrange("p e n -> p n e")
            )

        def cs(i):
            u, c0, w, wv = CHUNKS[i]
            nc.scalar.activation(
                out=words[u][:, c0 + wv : c0 + w, :],
                in_=raw[i][:, :, wv:w].rearrange("p e n -> p n e"),
                func=ACT.Copy,
            )

        def g(b, u):
            nc.vector.tensor_copy(
                out=picked[b][:, u].rearrange("p n e -> p (n e)").bitcast(U32),
                in_=words[u][:].rearrange("p n e -> p (n e)").bitcast(U32).indirect(lists[b]),
            )

        def tv(b, u):
            t = psum.tile([P, 4, P], F32, name="turned", bufs=4)
            pairs = picked[b][:, u].rearrange("p n e -> p (n e)").bitcast(F32).rearrange("p (s j) -> p j s", j=4)
            for j in range(4):
                nc.tensor.transpose(t[:, j, :], pairs[:, j, :], ident_f[:])
            turned[b, u] = t

        def vc(b, u):
            nc.scalar.copy(
                out=vals[b][:, u * 2 * P : (u + 1) * 2 * P, :].rearrange("s (e p) j -> s e p j", e=2),
                in_=turned[b, u][:].rearrange("s j p -> s (j p)").bitcast(BF16).rearrange("s (j p e) -> s e p j", j=4, e=2),
            )

        def qv(b):
            if "vq" not in vqs:
                vqs["vq"] = keep.tile([P, B, DV], U32, name="vq", tag="toks", align_bytes=64)
                vqs["vs"] = keep.tile([P, B, DV], U8, name="vs", align_bytes=64)
            nc.vector.quantize_mx(
                out=vqs["vq"][:, b, :].bitcast(FP8X4),
                scales=vqs["vs"][:, b, :],
                in_=vals[b][:].rearrange("p c j -> p (c j)"),
            )

        def qc(b):
            nc.scalar.activation(out=q_sb[:, b], in_=q_raw[:, b].rearrange("p t q -> p q t"), func=ACT.Copy)

        def qQ():
            nc.vector.quantize_mx(
                out=qq[:].bitcast(FP8X4), scales=qs[:], in_=q_sb[:].rearrange("p b q t -> p (b q t)")
            )

        def ilv(b):
            if b == 0:
                nc.vector.tensor_copy(
                    out=keys[b][:].rearrange("p n u e -> p (n u e)").bitcast(F32).rearrange("p (n u) -> p n u", u=2),
                    in_=picked[b][:].rearrange("p u n e -> p (u n e)").bitcast(F32).rearrange("p (u n) -> p n u", u=2),
                )
            else:
                nc.scalar.copy(out=keys[b][:], in_=picked[b][:].rearrange("p u n e -> p n u e"))

        def qK(b):
            nc.vector.quantize_mx(
                out=kq[b][:].bitcast(FP8X4), scales=ks[b][:], in_=keys[b][:].rearrange("p n u e -> p (n u e)")
            )

        def mm(b):
            sc = psum.tile([P, N], F32, name="sc", tag="sc", bufs=2)
            nc.tensor.matmul_mx(
                out=sc[:],
                lhsT=qq[:, b * NQ : (b + 1) * NQ].bitcast(FP8X4),
                lhsT_scale=qs[:, b * NQ : (b + 1) * NQ],
                rhs=kq[b][:].bitcast(FP8X4),
                rhs_scale=ks[b][:],
                start=True,
                stop=True,
            )
            scores[b] = sc

        def tok(b):
            nc.vector.tensor_copy(out=toks[:, b, :], in_=ts_sb[:].indirect(lists[b]))

        def tt(b):
            t = psum.tile([P, 4, P], F32, name="tt", tag="pt", bufs=2)
            for j in range(4):
                nc.tensor.transpose(t[:, j, :], toks[:, b, :].rearrange("q (s j) -> q j s", j=4)[:, j, :], ident_f[:])
            tts[b] = t

        def tcl(b):
            tcol[b] = keep.tile([P, 4], F32, name=f"tcol{b}")
            nc.scalar.copy(out=tcol[b][:], in_=tts[b][:, :, 0])

        def sca(b):
            a[b] = keep.tile([P, N], F32, name=f"a{b}")
            nc.vector.tensor_tensor(out=a[b][:], in0=scores[b][:], in1=toks[:, b, :], op=ALU.mult)

        def mx(b):
            neg_m[b] = keep.tile([P, 1], F32, name=f"nm{b}")
            nc.vector.tensor_reduce(
                out=neg_m[b][:],
                in_=a[b][:],
                axis=mybir.AxisListType.X,
                op=ALU.max,
                negate=True,
            )

        def ex(b):
            p[b] = keep.tile([P, 4, P], F32, name=f"p{b}")
            total[b] = keep.tile([P, 1], F32, name=f"total{b}")
            nc.scalar.activation(
                out=p[b][:].rearrange("q j s -> q s j"),
                in_=a[b][:].rearrange("q (s j) -> q s j", j=4),
                func=ACT.Exp,
                bias=neg_m[b][:],
                scale=1.0,
                accum_out=total[b][:],
            )

        def pt(b):
            t = psum.tile([P, 4, P], F32, name="pt", tag="pt", bufs=2)
            for j in range(4):
                nc.tensor.transpose(t[:, j, :], p[b][:, j, :], ident_f[:])
            pts[b] = t

        def w(b):
            wts[b] = keep.tile([P, NQ, 4], BF16, name=f"w{b}", align_bytes=64)
            nc.vector.tensor_tensor(
                out=wts[b][:],
                in0=pts[b][:].rearrange("s j q -> s q j"),
                in1=tcol[b][:].unsqueeze(1).to_broadcast([P, NQ, 4]),
                op=ALU.mult,
            )

        def qw(b):
            wq = keep.tile([P, NQ], U32, name=f"wq{b}", align_bytes=64)
            ws = keep.tile([P, NQ], U8, name=f"ws{b}", align_bytes=64)
            nc.vector.quantize_mx(out=wq[:].bitcast(FP8X4), scales=ws[:], in_=wts[b][:].rearrange("s q j -> s (q j)"))
            wqs[b] = (wq, ws)

        def rec(b):
            invs[b] = keep.tile([P, 1], F32, name=f"inv{b}")
            nc.vector.reciprocal(out=invs[b][:], in_=total[b][:])

        def mix(b):
            wq, ws = wqs[b]
            ys[b] = psum.tile([P, DV], F32, name="y", tag="sc", bufs=2)
            nc.tensor.matmul_mx(
                out=ys[b][:],
                lhsT=wq[:].bitcast(FP8X4),
                lhsT_scale=ws[:],
                rhs=vqs["vq"][:, b, :].bitcast(FP8X4),
                rhs_scale=vqs["vs"][:, b, :],
                start=True,
                stop=True,
            )

        def fin(b):
            o = keep.tile([P, DV], F32, name=f"o{b}")
            nc.vector.scalar_tensor_tensor(
                out=o[:].rearrange("q (p f) -> q p f", f=4),
                in0=ys[b][:].rearrange("q (f p) -> q p f", f=4),
                scalar=invs[b][:],
                in1=ch_sb[:].rearrange("q (p f) -> q p f", f=4),
                op0=ALU.mult,
                op1=ALU.mult,
            )
            nc.sync.dma_start(out=out[b], in_=o[:])

        cv(0)
        cs(0)
        cv(1)
        cs(1)
        g(0, 0)
        cs(2)
        g(1, 0)
        tv(0, 0)
        vc(0, 0)
        cv(3)
        tv(1, 0)
        vc(1, 0)
        cv(4)
        qc(0)
        qc(1)
        g(0, 1)
        g(1, 1)
        ilv(1)
        ilv(0)
        tv(0, 1)
        vc(0, 1)
        tv(1, 1)
        vc(1, 1)
        qQ()
        qK(0)
        mm(0)
        qK(1)
        mm(1)
        tok(0)
        tt(0)
        tcl(0)
        tok(1)
        tt(1)
        tcl(1)
        sca(0)
        sca(1)
        mx(0)
        ex(0)
        mx(1)
        ex(1)
        pt(0)
        rec(0)
        w(0)
        pt(1)
        qw(0)
        qv(0)
        mix(0)
        w(1)
        rec(1)
        qw(1)
        qv(1)
        mix(1)
        fin(0)
        fin(1)
